import numpy as np
import ml_dtypes


def mxq(x, axis, fmt="e4m3"):
    dtype, down = {"e4m3": (ml_dtypes.float8_e4m3fn, 7), "e5m2": (ml_dtypes.float8_e5m2, 14)}[fmt]
    v = np.moveaxis(np.asarray(x, np.float32).astype(ml_dtypes.bfloat16).astype(np.float64), axis, -1)
    blocks = v.reshape(v.shape[:-1] + (-1, 32))
    amax = np.abs(blocks).max(-1, keepdims=True)
    byte = np.maximum(np.where(amax > 0, np.frexp(amax)[1] - 1 + 127, 0) - down, 1)
    scale = np.exp2(byte - 127.0)
    codes = (blocks / scale).astype(np.float32).astype(dtype).astype(np.float64)
    return np.moveaxis((codes * scale).reshape(v.shape), -1, axis)


WIDE = False


def mx_kscale(k):
    if not WIDE:
        return np.ones(k)
    levels = np.array([30, -30])
    if k % 512:
        return np.exp2(np.random.permutation(np.resize(levels, k // 32))).repeat(32)
    a = np.empty((k // 512, 16))
    for p in range(k // 512):
        a[p, :8] = np.random.permutation(np.resize(levels, 8))
        for g in range(8):
            far = levels[np.abs(levels - a[p, g]) >= 10]
            a[p, g + 8] = far[np.random.randint(len(far))]
    return np.exp2(a.ravel()).repeat(32)


BF16 = ml_dtypes.bfloat16


def bf(x):
    return np.asarray(x, np.float32).astype(BF16)


def f64(x):
    return np.asarray(x).astype(np.float64)


E2M1 = np.array([0.0, 0.5, 1.0, 1.5, 2.0, 3.0, 4.0, 6.0, -0.0, -0.5, -1.0, -1.5, -2.0, -3.0, -4.0, -6.0])


def pack_weight(w, fmt):
    k, n = w.shape
    w = f64(bf(w)).reshape(k // 32, 32, n)
    amax = np.abs(w).max(1)
    if fmt == "e4m3":
        byte = np.frexp(amax)[1] - 1 + 127 - 7
    else:
        mant, ex = np.frexp(amax / 6.0)
        byte = np.where(mant > 0.5, ex, ex - 1) + 127
    byte = np.clip(np.where(amax > 0, byte, 1), 1, 254)
    scaled = (w * np.exp2(127.0 - byte)[:, None, :]).reshape(k, n).astype(np.float32)
    by_word = np.ascontiguousarray(scaled.reshape(k // 512, 128, 4, n).transpose(0, 1, 3, 2))
    if fmt == "e4m3":
        words = by_word.astype(ml_dtypes.float8_e4m3fn).view(np.uint8)
    else:
        c = by_word.astype(ml_dtypes.float4_e2m1fn).view(np.uint8) & 0xF
        words = c[..., 0::2] | (c[..., 1::2] << 4)
    return np.ascontiguousarray(words), np.ascontiguousarray(byte.astype(np.uint8).reshape(k // 512, 16, n))


def unpack_weight(words, scales, fmt):
    g, p, n, _ = words.shape
    if fmt == "e4m3":
        vals = np.ascontiguousarray(words).view(ml_dtypes.float8_e4m3fn).astype(np.float64)
    else:
        nib = np.empty((g, p, n, 4), np.uint8)
        nib[..., 0::2] = words & 0xF
        nib[..., 1::2] = words >> 4
        vals = E2M1[nib]
    vals = vals * np.repeat(np.exp2(scales.astype(np.float64) - 127.0), 8, axis=1)[..., None]
    return vals.transpose(0, 1, 3, 2).reshape(g * 512, n)
def pack4(w):
    words, scales = pack_weight(w, "e2m1")
    return words.reshape(words.shape[0], 128, -1), scales


def unpack4(words, scales):
    return unpack_weight(words.reshape(words.shape[0], 128, -1, 2), scales, "e2m1")


T, L, D, E = 2048, 2048, 1024, 1024


def setup_inputs():
    s, u = mx_kscale(T), mx_kscale(D)
    v_words, v_scales = pack4(np.random.standard_normal((T, E)) / s[:, None])
    return {
        "keys": bf(np.random.standard_normal((T, D)) / np.sqrt(T) * s[:, None] * u),
        "key_decay": bf(np.random.uniform(0.5, 1.0, T)),
        "v_words": v_words,
        "v_scales": v_scales,
        "state": bf(np.random.standard_normal((D, E)) * u[:, None]),
        "state_decay": bf(np.random.uniform(0.4, 0.95, D)),
        "queries": bf(np.random.standard_normal((L, D)) / np.sqrt(D) / u),
        "read_decay": bf(np.random.uniform(0.5, 1.0, L)),
    }


def reference(keys, key_decay, v_words, v_scales, state, state_decay, queries, read_decay):
    kd = f64(keys) * f64(key_decay)[:, None]
    values = unpack4(v_words, v_scales)
    write = mxq(kd, 0, "e4m3").T @ values
    new_state = f64(state_decay)[:, None] * f64(state) + write
    read = mxq(f64(queries), 1, "e4m3") @ mxq(new_state, 0, "e5m2")
    return f64(read_decay)[:, None] * read, new_state

@@ -1,0 +1,250 @@
+from contextlib import ExitStack
+
+import concourse.mybir as mybir
+from concourse.masks import make_identity
+
+T, L, D, E = 2048, 2048, 1024, 1024
+FLOPS = 2 * T * D * E + 2 * L * D * E
+
+F32 = mybir.dt.float32
+BF16 = mybir.dt.bfloat16
+I32 = mybir.dt.int32
+U32 = mybir.dt.uint32
+U8 = mybir.dt.uint8
+E4M3 = mybir.dt.float8_e4m3fn_x4
+E5M2 = mybir.dt.float8_e5m2_x4
+E2M1 = mybir.dt.float4_e2m1fn_x4
+MULT = mybir.AluOpType.mult
+ADD = mybir.AluOpType.add
+COPY = mybir.ActivationFunctionType.Copy
+
+P = 128
+TG = T // 512
+DG = D // 512
+HALF = 512
+LT = L // P
+LOADS = """k0_0 k0_2 v0 k1 k2 v1 k3 q3_0 v2 v3 s0 q2_2 q0_0 s1 q3_2 q1_2 q2_0 q1_0 q0_2"""
+ORDER = """M00 M01 M02 M03 I00s34 I01s24 I00v03 I01v02 M10 M11 M12 M13 K00 P0000 P0010 P0020 P0030 P0001 P0011 P0021 P0031 I10s14 I10v01 M20 M21 M22 M23 K10 P1000 P1010 P1020 P1030 P1001 P1011 P1021 P1031 I20s24 I20v02 M30 M31 M32 M33 I11s04 K20 P2000 P2010 P2020 P2030 P2001 P2011 P2021 P2031 K01 I30s34 I30v03 K30 K11 P3000 P3010 P3020 P3030 P3001 P3011 P3021 P3031 F000 F010 I21s04 K21 F020 F030 R00g02 R00g24 P0100 P1100 P2100 F001 I31s04 F011 F021 P0120 P1120 P2120 P0110 P1110 P2110 F031 R01g02 R01g24 SN002 SN024 P0130 P1130 P2130 P0101 P1101 P2101 P0111 P1111 P2111 K31 P3100 P3110 P3120 P3130 P3101 P3111 P0121 P1121 P2121 P3121 N00 P0131 P1131 P2131 P3131 F100 F110 F120 F130 R10g02 R10g24 N01 F101 T0 F111 T1 F121 T2 F131 SN102 SN124 T3 T4 T5 C0s T6 C1s N10 T7 C2s T8 C3s Q0 T9 C4v T10 C5s Q1 T11 C6s T12 C7s Q2 T13 C8s R11g02 R11g24 N11 T14 C9v Q3 T15 C10s C11s Q4 C12s C13s Q5 C14v C15s Q6 Q7 X0_0 O0_0s X0_1 O0_1v SO0 X1_0 O1_0s X1_1 O1_1v SO1 X2_0 O2_0s X2_1 O2_1v SO2 X3_0 O3_0s X3_1 O3_1v SO3 X4_0 O4_0s X4_1 O4_1v SO4 X5_0 O5_0s X5_1 O5_1v SO5 X6_0 O6_0s X6_1 O6_1v SO6 X7_0 O7_0s X7_1 O7_1v SO7 X8_0 O8_0s X8_1 O8_1v SO8 X9_0 O9_0s X9_1 O9_1v SO9 X10_0 O10_0s X10_1 O10_1v SO10 X11_0 O11_0s X11_1 O11_1v SO11 X12_0 O12_0s X12_1 O12_1v SO12 X13_0 O13_0s X13_1 O13_1v SO13 X14_0 O14_0s X14_1 O14_1v SO14 X15_0 O15_0s X15_1 O15_1v SO15"""
+
+
+def tile_linear_attention_state_s9_kernel(
+    tc, keys, key_decay, v_words, v_scales, state, state_decay, queries, read_decay, out_0, out_1
+):
+    nc = tc.nc
+    with ExitStack() as ctx:
+        keep = ctx.enter_context(tc.tile_pool(name="keep", bufs=1))
+        stage = ctx.enter_context(tc.tile_pool(name="stage", bufs=4))
+        il = ctx.enter_context(tc.tile_pool(name="il", bufs=2))
+        qpool = ctx.enter_context(tc.tile_pool(name="qpool", bufs=3))
+        psum = ctx.enter_context(tc.psum_pool(name="psum", bufs=1))
+
+        kdec = keep.tile([P, TG, 4], BF16, name="kdec")
+        sdec = keep.tile([P, DG, 4], BF16, name="sdec")
+        rdec = keep.tile([P, 4, 4], BF16, name="rdec")
+        rdec32 = keep.tile([P, 4, 4], F32, name="rdec32")
+        dummy = keep.tile([P, 2], F32, name="dummy")
+        vsc = keep.tile([P, TG, E], U8, name="vsc", align_bytes=64)
+        ident = keep.tile([P, P], F32, name="ident", align_bytes=64)
+        st = keep.tile([P, DG, 4, E], BF16, name="st", align_bytes=64)
+        ns32 = keep.tile([P, DG, 4, E], F32, name="ns32", align_bytes=64)
+        kd_codes = keep.tile([P, TG, D], U32, name="kd_codes", align_bytes=64)
+        kd_scales = keep.tile([P, TG, D], U8, name="kd_scales", align_bytes=64)
+        q_codes = keep.tile([P, LT, DG, P], U32, name="q_codes", align_bytes=64)
+        q_scales = keep.tile([P, LT, DG, P], U8, name="q_scales", align_bytes=64)
+        ns_codes = keep.tile([P, DG, E], U32, name="ns_codes", align_bytes=64)
+        ns_scales = keep.tile([P, DG, E], U8, name="ns_scales", align_bytes=64)
+
+        keys_v = keys.rearrange("(g p j) d -> g p j d", p=P, j=4)
+        q_v = queries.rearrange("(c p r) d -> c p r d", p=P, r=4)
+        st_v = state.rearrange("(b p t) e -> b p t e", p=P, t=4)
+        out0_v = out_0.rearrange("(c p r) e -> c p r e", p=P, r=4)
+        out1_v = out_1.rearrange("(b p t) e -> b p t e", p=P, t=4)
+        kraw = []
+        vw = []
+        qraw = []
+        for g in range(TG):
+            kr = stage.tile([P, 4, D], BF16, name="raw", align_bytes=64)
+            kraw.append(kr)
+            w = keep.tile([P, 2 * E], U8, name=f"vw{g}", align_bytes=64)
+            vw.append(w)
+        for c in range(4):
+            qr = keep.tile([P, 4, D], BF16, name=f"qraw{c}", align_bytes=64)
+            qraw.append(qr)
+
+        with tc.manual_schedule():
+            nc.scalar.dma_start(out=kdec[:], in_=key_decay.rearrange("(g p j) -> p g j", p=P, j=4))
+            nc.vector.memset(dummy[:], 0.0)
+            nc.vector.memset(vsc[:].rearrange("p g n -> p (g n)").bitcast(I32), 0)
+            nc.scalar.activation(out=dummy[:, 1:2], in_=dummy[:, 0:1], func=COPY)
+            make_identity(nc, ident[:])
+            for name in LOADS.split():
+                i = int(name[1:2])
+                if name[0:1] == "v":
+                    nc.sync.dma_start(out=vw[i][:].bitcast(I32), in_=v_words[i].bitcast(I32))
+                elif name[0:1] == "s":
+                    nc.sync.dma_start(out=st[:, i], in_=st_v[i])
+                else:
+                    tiles, view = (kraw, keys_v) if name[0:1] == "k" else (qraw, q_v)
+                    rows = slice(int(name[3:4]), int(name[3:4]) + 2) if len(name) > 2 else slice(0, 4)
+                    nc.sync.dma_start(out=tiles[i][:, rows, :], in_=view[i, :, rows, :])
+            for q in range(4):
+                nc.scalar.dma_start(
+                    out=vsc[32 * q : 32 * q + 4].bitcast(I32),
+                    in_=v_scales[:, 4 * q : 4 * q + 4, :].rearrange("g q n -> q g n").bitcast(I32),
+                )
+            nc.scalar.dma_start(out=sdec[:], in_=state_decay.rearrange("(b p t) -> p b t", p=P, t=4))
+            nc.scalar.dma_start(out=rdec[:], in_=read_decay.rearrange("(c p r) -> p c r", p=P, r=4))
+
+            free_banks = list(range(8))
+            bank_of = {}
+            acc_of = {}
+            il_of = {}
+            res_of = {}
+
+            def take(key):
+                k = free_banks.pop(0)
+                bank_of[key] = k
+                acc = psum.tile([P, HALF], F32, name=f"bank{k}")
+                acc_of[key] = acc
+                return acc
+
+            for tok in ORDER.split():
+                c = tok[0:1]
+                if c == "M":
+                    g, j = int(tok[1:2]), int(tok[2:3])
+                    nc.vector.tensor_scalar(
+                        out=kraw[g][:, j, :], in0=kraw[g][:, j, :], scalar1=kdec[:, g, j : j + 1], scalar2=None, op0=MULT
+                    )
+                elif c == "I":
+                    g, b, e, lo, hi = int(tok[1:2]), int(tok[2:3]), tok[3:4], int(tok[4:5]), int(tok[5:6])
+                    if (g, b) not in il_of:
+                        grouped = il.tile([P, 4, P, 4], BF16, name=f"kd_il{b}", align_bytes=64)
+                        il_of[(g, b)] = grouped
+                    src = kraw[g][:, :, 512 * b : 512 * b + 512].rearrange("p j (m t) -> p m t j", t=4)[:, :, lo:hi, :]
+                    dst = il_of[(g, b)][:].rearrange("p t m j -> p m t j")[:, :, lo:hi, :]
+                    if e == "s":
+                        nc.scalar.copy(out=dst, in_=src)
+                    else:
+                        nc.vector.tensor_copy(out=dst, in_=src)
+                elif c == "K":
+                    g, b = int(tok[1:2]), int(tok[2:3])
+                    cols = slice(512 * b, 512 * b + 512)
+                    nc.vector.quantize_mx(
+                        out=kd_codes[:, g, cols].bitcast(E4M3),
+                        scales=kd_scales[:, g, cols],
+                        in_=il_of[(g, b)][:].rearrange("p t m j -> p (t m j)"),
+                    )
+                elif c == "P":
+                    g, b, t, h = int(tok[1:2]), int(tok[2:3]), int(tok[3:4]), int(tok[4:5])
+                    key = ("a", b, t, h)
+                    acc = take(key) if g == 0 else acc_of[key]
+                    cols = slice(512 * b + P * t, 512 * b + P * t + P)
+                    nc.tensor.matmul_mx(
+                        out=acc[:],
+                        lhsT=kd_codes[:, g, cols].bitcast(E4M3),
+                        lhsT_scale=kd_scales[:, g, cols],
+                        rhs=vw[g][:, 2 * HALF * h : 2 * HALF * (h + 1)].bitcast(E2M1),
+                        rhs_scale=vsc[:, g, HALF * h : HALF * (h + 1)],
+                        start=(g == 0),
+                        stop=(g == TG - 1),
+                    )
+                elif c == "T":
+                    l = int(tok[1:])
+                    words = qraw[l // 4][:, l % 4, :].bitcast(F32)
+                    bank = take(("t", l))
+                    for b in range(DG):
+                        for u in range(2):
+                            col = P * (2 * b + u)
+                            nc.tensor.transpose(
+                                bank[:, col : col + P], words[:, 256 * b + u : 256 * (b + 1) : 2], ident[:]
+                            )
+                elif c == "C":
+                    l, e = int(tok[1:-1]), tok[-1]
+                    if ("q", l // 2) not in il_of:
+                        pair = qpool.tile([P, 2, DG, P, 4], BF16, name="q_il", align_bytes=64)
+                        il_of[("q", l // 2)] = pair
+                    pair = il_of[("q", l // 2)]
+                    dst = pair[:, l % 2].rearrange("p b r t -> p (b r t)").bitcast(F32)
+                    dst = dst.rearrange("p (b r u) -> p b r u", b=DG, u=2)
+                    src = acc_of[("t", l)][:].rearrange("p (b u r) -> p b r u", b=DG, u=2)
+                    if e == "s":
+                        nc.scalar.copy(out=dst, in_=src)
+                    else:
+                        nc.vector.tensor_copy(out=dst, in_=src)
+                    free_banks.append(bank_of[("t", l)])
+                elif c == "Q":
+                    i = int(tok[1:])
+                    nc.vector.quantize_mx(
+                        out=q_codes[:, 2 * i : 2 * i + 2].rearrange("p l b r -> p (l b r)").bitcast(E4M3),
+                        scales=q_scales[:, 2 * i : 2 * i + 2].rearrange("p l b r -> p (l b r)"),
+                        in_=il_of[("q", i)][:].rearrange("p l b r t -> p (l b r t)"),
+                    )
+                elif c == "F":
+                    b, t, h = int(tok[1:2]), int(tok[2:3]), int(tok[3:4])
+                    cols = slice(HALF * h, HALF * (h + 1))
+                    nc.vector.scalar_tensor_tensor(
+                        out=ns32[:, b, t, cols],
+                        in0=st[:, b, t, cols],
+                        scalar=sdec[:, b, t : t + 1],
+                        in1=acc_of[("a", b, t, h)][:],
+                        op0=MULT,
+                        op1=ADD,
+                    )
+                    free_banks.append(bank_of[("a", b, t, h)])
+                elif c == "R":
+                    b, h, e, lo, hi = int(tok[1:2]), int(tok[2:3]), tok[3:4], int(tok[4:5]), int(tok[5:6])
+                    if ("n", b, h) not in il_of:
+                        grouped = il.tile([P, HALF, 4], BF16, name="ns_il", align_bytes=64)
+                        il_of[("n", b, h)] = grouped
+                    dst = il_of[("n", b, h)][:, P * lo : P * hi, :]
+                    src = ns32[:, b, :, HALF * h + P * lo : HALF * h + P * hi].rearrange("p t n -> p n t")
+                    if e == "s":
+                        nc.scalar.copy(out=dst, in_=src)
+                    elif e == "v":
+                        nc.vector.tensor_copy(out=dst, in_=src)
+                    else:
+                        nc.gpsimd.tensor_scalar(out=dst, in0=src, scalar1=1.0, scalar2=0.0, op0=MULT, op1=ADD)
+                elif c == "N":
+                    b, h = int(tok[1:2]), int(tok[2:3])
+                    cols = slice(HALF * h, HALF * (h + 1))
+                    nc.vector.quantize_mx(
+                        out=ns_codes[:, b, cols].bitcast(E5M2),
+                        scales=ns_scales[:, b, cols],
+                        in_=il_of[("n", b, h)][:].rearrange("p n t -> p (n t)"),
+                    )
+                elif c == "X":
+                    l, h = int(tok[1:].split("_")[0]), int(tok[1:].split("_")[1])
+                    cols = slice(HALF * h, HALF * (h + 1))
+                    acc = take(("x", l, h))
+                    for b in range(DG):
+                        nc.tensor.matmul_mx(
+                            out=acc[:],
+                            lhsT=q_codes[:, l, b, :].bitcast(E4M3),
+                            lhsT_scale=q_scales[:, l, b, :],
+                            rhs=ns_codes[:, b, cols].bitcast(E5M2),
+                            rhs_scale=ns_scales[:, b, cols],
+                            start=(b == 0),
+                            stop=(b == DG - 1),
+                        )
+                elif c == "O":
+                    l, h, e = int(tok[1:].split("_")[0]), int(tok[-2:-1]), tok[-1]
+                    cols = slice(HALF * h, HALF * (h + 1))
+                    if l == 0 and h == 0:
+                        nc.vector.tensor_copy(out=rdec32[:], in_=rdec[:])
+                    if l // 2 not in res_of:
+                        res = stage.tile([P, 2, E], F32, name="raw", align_bytes=64)
+                        res_of[l // 2] = res
+                    factor = rdec32[:, l // 4, l % 4 : l % 4 + 1]
+                    if e == "s":
+                        nc.scalar.activation(out=res_of[l // 2][:, l % 2, cols], in_=acc_of[("x", l, h)][:], func=COPY, scale=factor)
+                    else:
+                        nc.vector.tensor_scalar(
+                            out=res_of[l // 2][:, l % 2, cols], in0=acc_of[("x", l, h)][:], scalar1=factor, scalar2=None, op0=MULT
+                        )
+                    free_banks.append(bank_of[("x", l, h)])
+                elif tok[0:2] == "SO":
+                    l = int(tok[2:])
+                    nc.sync.dma_start(out=out0_v[l // 4, :, l % 4, :], in_=res_of[l // 2][:, l % 2, :])
+                else:
+                    b, lo, hi = int(tok[2:3]), int(tok[3:4]), int(tok[4:5])
+                    nc.sync.dma_start(out=out1_v[b, :, lo:hi, :], in_=ns32[:, b, lo:hi, :])

@@ -23,8 +23,8 @@ TG = T // 512
 DG = D // 512
 HALF = 512
 LT = L // P
-LOADS = """k0_0 k0_2 v0 k1 k2 v1 k3 q3_0 v2 v3 s0 q2_2 q0_0 s1 q3_2 q1_2 q2_0 q1_0 q0_2"""
-ORDER = """M00 M01 M02 M03 I00s34 I01s24 I00v03 I01v02 M10 M11 M12 M13 K00 P0000 P0010 P0020 P0030 P0001 P0011 P0021 P0031 I10s14 I10v01 M20 M21 M22 M23 K10 P1000 P1010 P1020 P1030 P1001 P1011 P1021 P1031 I20s24 I20v02 M30 M31 M32 M33 I11s04 K20 P2000 P2010 P2020 P2030 P2001 P2011 P2021 P2031 K01 I30s34 I30v03 K30 K11 P3000 P3010 P3020 P3030 P3001 P3011 P3021 P3031 F000 F010 I21s04 K21 F020 F030 R00g02 R00g24 P0100 P1100 P2100 F001 I31s04 F011 F021 P0120 P1120 P2120 P0110 P1110 P2110 F031 R01g02 R01g24 SN002 SN024 P0130 P1130 P2130 P0101 P1101 P2101 P0111 P1111 P2111 K31 P3100 P3110 P3120 P3130 P3101 P3111 P0121 P1121 P2121 P3121 N00 P0131 P1131 P2131 P3131 F100 F110 F120 F130 R10g02 R10g24 N01 F101 T0 F111 T1 F121 T2 F131 SN102 SN124 T3 T4 T5 C0s T6 C1s N10 T7 C2s T8 C3s Q0 T9 C4v T10 C5s Q1 T11 C6s T12 C7s Q2 T13 C8s R11g02 R11g24 N11 T14 C9v Q3 T15 C10s C11s Q4 C12s C13s Q5 C14v C15s Q6 Q7 X0_0 O0_0s X0_1 O0_1v SO0 X1_0 O1_0s X1_1 O1_1v SO1 X2_0 O2_0s X2_1 O2_1v SO2 X3_0 O3_0s X3_1 O3_1v SO3 X4_0 O4_0s X4_1 O4_1v SO4 X5_0 O5_0s X5_1 O5_1v SO5 X6_0 O6_0s X6_1 O6_1v SO6 X7_0 O7_0s X7_1 O7_1v SO7 X8_0 O8_0s X8_1 O8_1v SO8 X9_0 O9_0s X9_1 O9_1v SO9 X10_0 O10_0s X10_1 O10_1v SO10 X11_0 O11_0s X11_1 O11_1v SO11 X12_0 O12_0s X12_1 O12_1v SO12 X13_0 O13_0s X13_1 O13_1v SO13 X14_0 O14_0s X14_1 O14_1v SO14 X15_0 O15_0s X15_1 O15_1v SO15"""
+LOADS = """k0_0 k0_2 v0 k1 sc q0_0 k2 v1 k3 q3_0 v2 v3 s0 q1_0 q2_0 s1 q1_2 q2_2 q0_2 q3_2"""
+ORDER = """M00 M01 M02 M03 I01s24 I01v02 I00s14 I00v01 T0 K01 T1 M10 M11 M12 M13 I10s24 I10v02 K00 C0s C1s P0000 P0010 P0020 P0030 P0001 P0011 P0021 P0031 K10 P1000 P1010 P1020 P1030 P1001 P1011 P1021 P1031 M20 M21 M22 M23 Q0 I20s24 I21s04 I20v02 M30 M31 M32 M33 K20 P2000 P2010 P2020 P2030 P2001 P2011 P2021 P2031 I30v04 K30 P3000 P3010 P3020 P3030 P3001 P3011 P3021 P3031 K21 F000 I11s04 K11 F010 F020 I31s04 P0100 P1100 P2100 F030 P0110 P1110 P2110 F001 P0120 P1120 P2120 F011 P0101 P1101 P2101 F021 P0130 P1130 P2130 K31 P3100 P3110 P3120 P3130 P3101 F031 SN002 SN024 R00s04 F100 P0111 P1111 P2111 P3111 F110 N00 F120 F130 R01s04 N01 P0121 P1121 P2121 P3121 F101 F111 T2 R10s04 F121 T3 P0131 P1131 P2131 P3131 T4 C2s F131 SN102 SN124 T5 C3s N10 T6 T7 C4v R11s02 R11v24 N11 X0_0 T8 Q1 O0_0s T9 C5s C6s T10 C7s T11 C8s X0_1 Q2 T12 C9v O0_1v SO0 T13 Q3 C10s T14 C11s T15 Q4 C12s X1_0 C13s O1_0s Q5 C14v C15s Q6 X1_1 O1_1v SO1 Q7 X2_0 O2_0s X2_1 O2_1v SO2 X3_0 O3_0s X3_1 O3_1v SO3 X4_0 O4_0s X4_1 O4_1v SO4 X5_0 O5_0s X5_1 O5_1v SO5 X6_0 O6_0s X6_1 O6_1v SO6 X7_0 O7_0s X7_1 O7_1v SO7 X8_0 O8_0s X8_1 O8_1v SO8 X9_0 O9_0s X9_1 O9_1v SO9 X10_0 O10_0s X10_1 O10_1v SO10 X11_0 O11_0s X11_1 O11_1v SO11 X12_0 O12_0s X12_1 O12_1v SO12 X13_0 O13_0s X13_1 O13_1v SO13 X14_0 O14_0s X14_1 O14_1v SO14 X15_0 O15_0s X15_1 O15_1v SO15"""
 
 
 def tile_linear_attention_state_s9_kernel(
@@ -38,9 +38,8 @@ def tile_linear_attention_state_s9_kernel(
         qpool = ctx.enter_context(tc.tile_pool(name="qpool", bufs=3))
         psum = ctx.enter_context(tc.psum_pool(name="psum", bufs=1))
 
-        kdec = keep.tile([P, TG, 4], BF16, name="kdec")
-        sdec = keep.tile([P, DG, 4], BF16, name="sdec")
-        rdec = keep.tile([P, 4, 4], BF16, name="rdec")
+        dec_rows = keep.tile([P, 512], BF16, name="dec_rows", align_bytes=64)
+        dec = keep.tile([P, 10, 4], BF16, name="dec", align_bytes=64)
         rdec32 = keep.tile([P, 4, 4], F32, name="rdec32")
         dummy = keep.tile([P, 2], F32, name="dummy")
         vsc = keep.tile([P, TG, E], U8, name="vsc", align_bytes=64)
@@ -72,14 +71,23 @@ def tile_linear_attention_state_s9_kernel(
             qraw.append(qr)
 
         with tc.manual_schedule():
-            nc.scalar.dma_start(out=kdec[:], in_=key_decay.rearrange("(g p j) -> p g j", p=P, j=4))
+            nc.vector.memset(dec_rows[:].bitcast(I32), 0)
+            nc.scalar.dma_start(out=dec_rows[0:4, :], in_=key_decay.rearrange("(g n) -> g n", n=512))
+            nc.scalar.dma_start(out=dec_rows[4:6, :], in_=state_decay.rearrange("(g n) -> g n", n=512))
+            nc.scalar.dma_start(out=dec_rows[6:10, :], in_=read_decay.rearrange("(g n) -> g n", n=512))
             nc.vector.memset(dummy[:], 0.0)
             nc.vector.memset(vsc[:].rearrange("p g n -> p (g n)").bitcast(I32), 0)
             nc.scalar.activation(out=dummy[:, 1:2], in_=dummy[:, 0:1], func=COPY)
             make_identity(nc, ident[:])
             for name in LOADS.split():
-                i = int(name[1:2])
-                if name[0:1] == "v":
+                i = int(name[1:2]) if name != "sc" else 0
+                if name == "sc":
+                    for q in range(4):
+                        nc.sync.dma_start(
+                            out=vsc[32 * q : 32 * q + 4].bitcast(I32),
+                            in_=v_scales[:, 4 * q : 4 * q + 4, :].rearrange("g q n -> q g n").bitcast(I32),
+                        )
+                elif name[0:1] == "v":
                     nc.sync.dma_start(out=vw[i][:].bitcast(I32), in_=v_words[i].bitcast(I32))
                 elif name[0:1] == "s":
                     nc.sync.dma_start(out=st[:, i], in_=st_v[i])
@@ -87,13 +95,6 @@ def tile_linear_attention_state_s9_kernel(
                     tiles, view = (kraw, keys_v) if name[0:1] == "k" else (qraw, q_v)
                     rows = slice(int(name[3:4]), int(name[3:4]) + 2) if len(name) > 2 else slice(0, 4)
                     nc.sync.dma_start(out=tiles[i][:, rows, :], in_=view[i, :, rows, :])
-            for q in range(4):
-                nc.scalar.dma_start(
-                    out=vsc[32 * q : 32 * q + 4].bitcast(I32),
-                    in_=v_scales[:, 4 * q : 4 * q + 4, :].rearrange("g q n -> q g n").bitcast(I32),
-                )
-            nc.scalar.dma_start(out=sdec[:], in_=state_decay.rearrange("(b p t) -> p b t", p=P, t=4))
-            nc.scalar.dma_start(out=rdec[:], in_=read_decay.rearrange("(c p r) -> p c r", p=P, r=4))
 
             free_banks = list(range(8))
             bank_of = {}
@@ -108,20 +109,30 @@ def tile_linear_attention_state_s9_kernel(
                 acc_of[key] = acc
                 return acc
 
+            bank = take("dec")
+            for u in range(2):
+                nc.tensor.transpose(bank[:, P * u : P * u + P], dec_rows[:].bitcast(F32)[:, u:256:2], ident[:])
+            nc.vector.tensor_copy(
+                out=dec[:].rearrange("p r j -> p (r j)").bitcast(F32).rearrange("p (r u) -> p r u", u=2),
+                in_=bank[:, 0 : 2 * P].rearrange("p (u r) -> p r u", u=2)[:, 0:10, :],
+            )
+            free_banks.append(bank_of["dec"])
+            nc.vector.tensor_copy(out=rdec32[:], in_=dec[:, 6:10, :])
+
             for tok in ORDER.split():
                 c = tok[0:1]
                 if c == "M":
                     g, j = int(tok[1:2]), int(tok[2:3])
                     nc.vector.tensor_scalar(
-                        out=kraw[g][:, j, :], in0=kraw[g][:, j, :], scalar1=kdec[:, g, j : j + 1], scalar2=None, op0=MULT
+                        out=kraw[g][:, j, :], in0=kraw[g][:, j, :], scalar1=dec[:, g, j : j + 1], scalar2=None, op0=MULT
                     )
                 elif c == "I":
                     g, b, e, lo, hi = int(tok[1:2]), int(tok[2:3]), tok[3:4], int(tok[4:5]), int(tok[5:6])
                     if (g, b) not in il_of:
                         grouped = il.tile([P, 4, P, 4], BF16, name=f"kd_il{b}", align_bytes=64)
                         il_of[(g, b)] = grouped
-                    src = kraw[g][:, :, 512 * b : 512 * b + 512].rearrange("p j (m t) -> p m t j", t=4)[:, :, lo:hi, :]
-                    dst = il_of[(g, b)][:].rearrange("p t m j -> p m t j")[:, :, lo:hi, :]
+                    src = kraw[g][:, :, 512 * b : 512 * b + 512].rearrange("p j (m t) -> p t m j", t=4)[:, lo:hi]
+                    dst = il_of[(g, b)][:, lo:hi]
                     if e == "s":
                         nc.scalar.copy(out=dst, in_=src)
                     else:
@@ -185,7 +196,7 @@ def tile_linear_attention_state_s9_kernel(
                     nc.vector.scalar_tensor_tensor(
                         out=ns32[:, b, t, cols],
                         in0=st[:, b, t, cols],
-                        scalar=sdec[:, b, t : t + 1],
+                        scalar=dec[:, 4 + b, t : t + 1],
                         in1=acc_of[("a", b, t, h)][:],
                         op0=MULT,
                         op1=ADD,
@@ -229,8 +240,6 @@ def tile_linear_attention_state_s9_kernel(
                 elif c == "O":
                     l, h, e = int(tok[1:].split("_")[0]), int(tok[-2:-1]), tok[-1]
                     cols = slice(HALF * h, HALF * (h + 1))
-                    if l == 0 and h == 0:
-                        nc.vector.tensor_copy(out=rdec32[:], in_=rdec[:])
                     if l // 2 not in res_of:
                         res = stage.tile([P, 2, E], F32, name="raw", align_bytes=64)
                         res_of[l // 2] = res

@@ -23,8 +23,20 @@ TG = T // 512
 DG = D // 512
 HALF = 512
 LT = L // P
-LOADS = """k0_0 k0_2 v0 k1 sc q0_0 k2 v1 k3 q3_0 v2 v3 s0 q1_0 q2_0 s1 q1_2 q2_2 q0_2 q3_2"""
-ORDER = """M00 M01 M02 M03 I01s24 I01v02 I00s14 I00v01 T0 K01 T1 M10 M11 M12 M13 I10s24 I10v02 K00 C0s C1s P0000 P0010 P0020 P0030 P0001 P0011 P0021 P0031 K10 P1000 P1010 P1020 P1030 P1001 P1011 P1021 P1031 M20 M21 M22 M23 Q0 I20s24 I21s04 I20v02 M30 M31 M32 M33 K20 P2000 P2010 P2020 P2030 P2001 P2011 P2021 P2031 I30v04 K30 P3000 P3010 P3020 P3030 P3001 P3011 P3021 P3031 K21 F000 I11s04 K11 F010 F020 I31s04 P0100 P1100 P2100 F030 P0110 P1110 P2110 F001 P0120 P1120 P2120 F011 P0101 P1101 P2101 F021 P0130 P1130 P2130 K31 P3100 P3110 P3120 P3130 P3101 F031 SN002 SN024 R00s04 F100 P0111 P1111 P2111 P3111 F110 N00 F120 F130 R01s04 N01 P0121 P1121 P2121 P3121 F101 F111 T2 R10s04 F121 T3 P0131 P1131 P2131 P3131 T4 C2s F131 SN102 SN124 T5 C3s N10 T6 T7 C4v R11s02 R11v24 N11 X0_0 T8 Q1 O0_0s T9 C5s C6s T10 C7s T11 C8s X0_1 Q2 T12 C9v O0_1v SO0 T13 Q3 C10s T14 C11s T15 Q4 C12s X1_0 C13s O1_0s Q5 C14v C15s Q6 X1_1 O1_1v SO1 Q7 X2_0 O2_0s X2_1 O2_1v SO2 X3_0 O3_0s X3_1 O3_1v SO3 X4_0 O4_0s X4_1 O4_1v SO4 X5_0 O5_0s X5_1 O5_1v SO5 X6_0 O6_0s X6_1 O6_1v SO6 X7_0 O7_0s X7_1 O7_1v SO7 X8_0 O8_0s X8_1 O8_1v SO8 X9_0 O9_0s X9_1 O9_1v SO9 X10_0 O10_0s X10_1 O10_1v SO10 X11_0 O11_0s X11_1 O11_1v SO11 X12_0 O12_0s X12_1 O12_1v SO12 X13_0 O13_0s X13_1 O13_1v SO13 X14_0 O14_0s X14_1 O14_1v SO14 X15_0 O15_0s X15_1 O15_1v SO15"""
+LOADS = """k0_0 k0_2 k1 V0 sa k2 sb k3 V2 s0 q0_2 q1 q0_0 s1 q2 q3"""
+ORDER = """m00 m20 m10 m30 D0 m01 m11 m21 m31 I00v04 I01s04 M10 M11 M12 K00 M13 P0000 P0010 P0020 P0030 I10v04 I11s04 M20
+M21 M22 M23 K01 K10 I20s24 I20v02 P0001 P0011 P0021 P0031 P1000 P1010 P1020 P1030 P1001 P1011 P1021 P1031 M30
+M31 M32 M33 K20 I30v04 P2000 P2010 P2020 P2030 P2001 P2011 P2021 P2031 K30 K11 I21s04 I31s04 W2s K21 P3001 P3000
+P3010 P3020 P3030 P3011 P3021 P3031 F001 F000 F010 F011 P0100 P1100 P0101 P2100 P1101 P0110 P2101 F021 F031 F020
+K31 W3s R01v34 R01s03 T2 T3 P0111 P3100 P3101 P0131 P1111 P1131 C2s C3s W0v W1v N01 F030 F101 P0121 P2131 P1121
+P3131 P2121 P2111 P3121 P1110 P3111 P2110 P0120 P0130 Q1 F131 F121 F111 W4s W5s W6s W7v T0 T1 T4 R11v04 R00s04
+SN024 F100 N11 C0s C1s C4s T5 P3110 P1130 P1120 P2130 P2120 P3130 C5s W8s W9s W10s Q0 Q2 X2_1 X0_1 F110 F130
+SN002 O0_1s P3120 F120 X1_1 X3_1 X4_1 W11v R10v34 R10s03 O2_1v O3_1v SN102 T6 T7 T8 T9 T11 C6s C7s N00 N10 O4_1s
+C8v C9s X5_1 X0_0 X5_0 X4_0 X1_0 SO2b SO3b O0_0v O5_0v O4_0v O5_1s Q3 Q4 W12v W13v W14v SN124 X2_0 X3_0 X6_0
+X6_1 C11s SO5 SO4 O1_0s O1_1s O2_0s O3_0s O6_0s O6_1s SO2a X7_0 X7_1 X8_0 W15v T10 T12 T13 T14 O7_0v O7_1s C10v
+C12v C13v SO0 SO1 Q5 T15 X8_1 X9_0 X9_1 X10_0 X10_1 O8_0v O8_1s O9_0s O9_1v C14s C15s SO3a SP3 X11_0 X11_1 SO8
+Q6 O10_0v O10_1s O11_0v X12_0 X12_1 X13_0 X13_1 Q7 X14_0 X14_1 X15_1 SO9 SO10 O12_0v O11_1s O12_1s O13_0v O13_1v
+O15_1v X15_0 SO11 SO12 SO13 O15_0v O14_0s O14_1s SO14 SO15"""
 
 
 def tile_linear_attention_state_s9_kernel(
@@ -35,11 +47,14 @@ def tile_linear_attention_state_s9_kernel(
         keep = ctx.enter_context(tc.tile_pool(name="keep", bufs=1))
         stage = ctx.enter_context(tc.tile_pool(name="stage", bufs=4))
         il = ctx.enter_context(tc.tile_pool(name="il", bufs=2))
+        nil = ctx.enter_context(tc.tile_pool(name="nil", bufs=4))
+        wpool = ctx.enter_context(tc.tile_pool(name="wpool", bufs=6))
         qpool = ctx.enter_context(tc.tile_pool(name="qpool", bufs=3))
         psum = ctx.enter_context(tc.psum_pool(name="psum", bufs=1))
 
         dec_rows = keep.tile([P, 512], BF16, name="dec_rows", align_bytes=64)
         dec = keep.tile([P, 10, 4], BF16, name="dec", align_bytes=64)
+        kdec0 = keep.tile([P, 4], BF16, name="kdec0", align_bytes=64)
         rdec32 = keep.tile([P, 4, 4], F32, name="rdec32")
         dummy = keep.tile([P, 2], F32, name="dummy")
         vsc = keep.tile([P, TG, E], U8, name="vsc", align_bytes=64)
@@ -59,38 +74,44 @@ def tile_linear_attention_state_s9_kernel(
         out0_v = out_0.rearrange("(c p r) e -> c p r e", p=P, r=4)
         out1_v = out_1.rearrange("(b p t) e -> b p t e", p=P, t=4)
         kraw = []
-        vw = []
+        vw = keep.tile([P, TG, 2 * E], U8, name="vw", align_bytes=64)
         qraw = []
         for g in range(TG):
             kr = stage.tile([P, 4, D], BF16, name="raw", align_bytes=64)
             kraw.append(kr)
-            w = keep.tile([P, 2 * E], U8, name=f"vw{g}", align_bytes=64)
-            vw.append(w)
         for c in range(4):
             qr = keep.tile([P, 4, D], BF16, name=f"qraw{c}", align_bytes=64)
             qraw.append(qr)
 
         with tc.manual_schedule():
+            nc.scalar.dma_start(out=kdec0[:], in_=key_decay[0:512].rearrange("(p j) -> p j", j=4))
+            nc.vector.memset(dummy[:], 0.0)
             nc.vector.memset(dec_rows[:].bitcast(I32), 0)
             nc.scalar.dma_start(out=dec_rows[0:4, :], in_=key_decay.rearrange("(g n) -> g n", n=512))
             nc.scalar.dma_start(out=dec_rows[4:6, :], in_=state_decay.rearrange("(g n) -> g n", n=512))
             nc.scalar.dma_start(out=dec_rows[6:10, :], in_=read_decay.rearrange("(g n) -> g n", n=512))
-            nc.vector.memset(dummy[:], 0.0)
             nc.vector.memset(vsc[:].rearrange("p g n -> p (g n)").bitcast(I32), 0)
             nc.scalar.activation(out=dummy[:, 1:2], in_=dummy[:, 0:1], func=COPY)
             make_identity(nc, ident[:])
             for name in LOADS.split():
-                i = int(name[1:2]) if name != "sc" else 0
-                if name == "sc":
+                i = int(name[1:2]) if name not in ("sa", "sb", "sc") else 0
+                if name in ("sa", "sb", "sc"):
+                    lo, hi = {"sa": (0, 1), "sb": (1, TG), "sc": (0, TG)}[name]
                     for q in range(4):
                         nc.sync.dma_start(
-                            out=vsc[32 * q : 32 * q + 4].bitcast(I32),
-                            in_=v_scales[:, 4 * q : 4 * q + 4, :].rearrange("g q n -> q g n").bitcast(I32),
+                            out=vsc[32 * q : 32 * q + 4, lo:hi, :].bitcast(I32),
+                            in_=v_scales[lo:hi, 4 * q : 4 * q + 4, :].rearrange("g q n -> q g n").bitcast(I32),
                         )
-                elif name[0:1] == "v":
-                    nc.sync.dma_start(out=vw[i][:].bitcast(I32), in_=v_words[i].bitcast(I32))
+                elif name[0:1] in ("v", "V"):
+                    end = i + 1 if name[0:1] == "v" else i + 2
+                    nc.sync.dma_start(
+                        out=vw[:, i:end, :].bitcast(I32), in_=v_words[i:end].rearrange("g p n -> p g n").bitcast(I32)
+                    )
                 elif name[0:1] == "s":
                     nc.sync.dma_start(out=st[:, i], in_=st_v[i])
+                elif name[-1] in ("L", "R"):
+                    cols = slice(0, 512) if name[-1] == "L" else slice(512, 1024)
+                    nc.sync.dma_start(out=kraw[0][:, :, cols], in_=keys_v[0, :, :, cols])
                 else:
                     tiles, view = (kraw, keys_v) if name[0:1] == "k" else (qraw, q_v)
                     rows = slice(int(name[3:4]), int(name[3:4]) + 2) if len(name) > 2 else slice(0, 4)
@@ -109,30 +130,43 @@ def tile_linear_attention_state_s9_kernel(
                 acc_of[key] = acc
                 return acc
 
-            bank = take("dec")
-            for u in range(2):
-                nc.tensor.transpose(bank[:, P * u : P * u + P], dec_rows[:].bitcast(F32)[:, u:256:2], ident[:])
-            nc.vector.tensor_copy(
-                out=dec[:].rearrange("p r j -> p (r j)").bitcast(F32).rearrange("p (r u) -> p r u", u=2),
-                in_=bank[:, 0 : 2 * P].rearrange("p (u r) -> p r u", u=2)[:, 0:10, :],
-            )
-            free_banks.append(bank_of["dec"])
-            nc.vector.tensor_copy(out=rdec32[:], in_=dec[:, 6:10, :])
 
             for tok in ORDER.split():
                 c = tok[0:1]
-                if c == "M":
-                    g, j = int(tok[1:2]), int(tok[2:3])
-                    nc.vector.tensor_scalar(
-                        out=kraw[g][:, j, :], in0=kraw[g][:, j, :], scalar1=dec[:, g, j : j + 1], scalar2=None, op0=MULT
+                if c == "D":
+                    bank = take("dec")
+                    for u in range(2):
+                        nc.tensor.transpose(bank[:, P * u : P * u + P], dec_rows[:].bitcast(F32)[:, u:256:2], ident[:])
+                    nc.vector.tensor_copy(
+                        out=dec[:].rearrange("p r j -> p (r j)").bitcast(F32).rearrange("p (r u) -> p r u", u=2),
+                        in_=bank[:, 0 : 2 * P].rearrange("p (u r) -> p r u", u=2)[:, 0:10, :],
                     )
+                    free_banks.append(bank_of["dec"])
+                    nc.vector.tensor_copy(out=rdec32[:], in_=dec[:, 6:10, :])
+                elif c == "m":
+                    j, b = int(tok[1:2]), int(tok[2:3])
+                    part = kraw[0][:, j, 512 * b : 512 * b + 512]
+                    nc.vector.tensor_scalar(out=part, in0=part, scalar1=kdec0[:, j : j + 1], scalar2=None, op0=MULT)
+                elif c == "M":
+                    g, j = int(tok[1:2]), int(tok[2:3])
+                    part = kraw[g][:, j, :]
+                    nc.vector.tensor_scalar(out=part, in0=part, scalar1=dec[:, g, j : j + 1], scalar2=None, op0=MULT)
                 elif c == "I":
                     g, b, e, lo, hi = int(tok[1:2]), int(tok[2:3]), tok[3:4], int(tok[4:5]), int(tok[5:6])
                     if (g, b) not in il_of:
                         grouped = il.tile([P, 4, P, 4], BF16, name=f"kd_il{b}", align_bytes=64)
                         il_of[(g, b)] = grouped
-                    src = kraw[g][:, :, 512 * b : 512 * b + 512].rearrange("p j (m t) -> p t m j", t=4)[:, lo:hi]
-                    dst = il_of[(g, b)][:, lo:hi]
+                    src = kraw[g][:, :, 512 * b : 512 * b + 512]
+                    dst = il_of[(g, b)][:]
+                    if e == "s":
+                        src = src.rearrange("p j (m t) -> p m j t", t=4)[:, :, :, lo:hi]
+                        dst = dst.rearrange("p t m j -> p m j t")[:, :, :, lo:hi]
+                    elif hi - lo == 4:
+                        src = src.rearrange("p j (m a c) -> p a m c j", a=2, c=2)
+                        dst = dst.rearrange("p (a c) m j -> p a m c j", a=2)
+                    else:
+                        src = src.rearrange("p j (m t) -> p t m j", t=4)[:, lo:hi]
+                        dst = dst[:, lo:hi]
                     if e == "s":
                         nc.scalar.copy(out=dst, in_=src)
                     else:
@@ -154,21 +188,33 @@ def tile_linear_attention_state_s9_kernel(
                         out=acc[:],
                         lhsT=kd_codes[:, g, cols].bitcast(E4M3),
                         lhsT_scale=kd_scales[:, g, cols],
-                        rhs=vw[g][:, 2 * HALF * h : 2 * HALF * (h + 1)].bitcast(E2M1),
+                        rhs=vw[:, g, 2 * HALF * h : 2 * HALF * (h + 1)].bitcast(E2M1),
                         rhs_scale=vsc[:, g, HALF * h : HALF * (h + 1)],
                         start=(g == 0),
                         stop=(g == TG - 1),
                     )
+                elif c == "W":
+                    l = int(tok[1:-1])
+                    perm = wpool.tile([P, DG, 2, P], F32, name="perm", align_bytes=64)
+                    il_of[("w", l)] = perm
+                    src = qraw[l // 4][:, l % 4, :].bitcast(F32).rearrange("p (b r u) -> p b u r", b=DG, u=2)
+                    if tok[-1] == "v":
+                        nc.vector.tensor_copy(out=perm[:], in_=src)
+                    else:
+                        nc.scalar.copy(out=perm[:], in_=src)
                 elif c == "T":
                     l = int(tok[1:])
                     words = qraw[l // 4][:, l % 4, :].bitcast(F32)
+                    perm = il_of.get(("w", l))
                     bank = take(("t", l))
                     for b in range(DG):
                         for u in range(2):
                             col = P * (2 * b + u)
-                            nc.tensor.transpose(
-                                bank[:, col : col + P], words[:, 256 * b + u : 256 * (b + 1) : 2], ident[:]
-                            )
+                            if perm is None:
+                                part = words[:, 256 * b + u : 256 * (b + 1) : 2]
+                            else:
+                                part = perm[:, b, u, :]
+                            nc.tensor.transpose(bank[:, col : col + P], part, ident[:])
                 elif c == "C":
                     l, e = int(tok[1:-1]), tok[-1]
                     if ("q", l // 2) not in il_of:
@@ -205,10 +251,12 @@ def tile_linear_attention_state_s9_kernel(
                 elif c == "R":
                     b, h, e, lo, hi = int(tok[1:2]), int(tok[2:3]), tok[3:4], int(tok[4:5]), int(tok[5:6])
                     if ("n", b, h) not in il_of:
-                        grouped = il.tile([P, HALF, 4], BF16, name="ns_il", align_bytes=64)
+                        grouped = nil.tile([P, HALF, 4], BF16, name="ns_il", align_bytes=64)
                         il_of[("n", b, h)] = grouped
                     dst = il_of[("n", b, h)][:, P * lo : P * hi, :]
-                    src = ns32[:, b, :, HALF * h + P * lo : HALF * h + P * hi].rearrange("p t n -> p n t")
+                    src = ns32[:, b, :, HALF * h + P * lo : HALF * h + P * hi]
+                    dst = dst.rearrange("p (n i) t -> p n t i", i=4)
+                    src = src.rearrange("p t (n i) -> p n t i", i=4)
                     if e == "s":
                         nc.scalar.copy(out=dst, in_=src)
                     elif e == "v":
@@ -251,9 +299,19 @@ def tile_linear_attention_state_s9_kernel(
                             out=res_of[l // 2][:, l % 2, cols], in0=acc_of[("x", l, h)][:], scalar1=factor, scalar2=None, op0=MULT
                         )
                     free_banks.append(bank_of[("x", l, h)])
+                elif tok[0:2] == "SP":
+                    i = int(tok[2:])
+                    nc.sync.dma_start(out=out0_v[i // 2, :, 2 * (i % 2) : 2 * (i % 2) + 2, :], in_=res_of[i][:])
+                elif tok[0:2] == "SH":
+                    b, h = int(tok[2:3]), int(tok[3:4])
+                    cols = slice(HALF * h, HALF * (h + 1))
+                    nc.sync.dma_start(out=out1_v[b, :, :, cols], in_=ns32[:, b, :, cols])
                 elif tok[0:2] == "SO":
-                    l = int(tok[2:])
-                    nc.sync.dma_start(out=out0_v[l // 4, :, l % 4, :], in_=res_of[l // 2][:, l % 2, :])
+                    l = int(tok[2:].replace("a", "").replace("b", ""))
+                    cols = slice(0, E)
+                    if tok[-1] in ("a", "b"):
+                        cols = slice(0, HALF) if tok[-1] == "a" else slice(HALF, E)
+                    nc.sync.dma_start(out=out0_v[l // 4, :, l % 4, cols], in_=res_of[l // 2][:, l % 2, cols])
                 else:
                     b, lo, hi = int(tok[2:3]), int(tok[3:4]), int(tok[4:5])
                     nc.sync.dma_start(out=out1_v[b, :, lo:hi, :], in_=ns32[:, b, lo:hi, :])

from contextlib import ExitStack

import concourse.mybir as mybir
from concourse.masks import make_identity

T, L, D, E = 2048, 2048, 1024, 1024
FLOPS = 2 * T * D * E + 2 * L * D * E

F32 = mybir.dt.float32
BF16 = mybir.dt.bfloat16
I32 = mybir.dt.int32
U32 = mybir.dt.uint32
U8 = mybir.dt.uint8
E4M3 = mybir.dt.float8_e4m3fn_x4
E5M2 = mybir.dt.float8_e5m2_x4
E2M1 = mybir.dt.float4_e2m1fn_x4
MULT = mybir.AluOpType.mult
ADD = mybir.AluOpType.add
COPY = mybir.ActivationFunctionType.Copy

P = 128
TG = T // 512
DG = D // 512
HALF = 512
LT = L // P
LOADS = """k0_0 k0_2 k1 V0 sa k2 sb k3 V2 s0 q0_2 q1 q0_0 s1 q2 q3"""
ORDER = """m00 m20 m10 m30 D0 m01 m11 m21 m31 I00v04 I01s04 M10 M11 M12 K00 M13 P0000 P0010 P0020 P0030 I10v04 I11s04 M20
M21 M22 M23 K01 K10 I20s24 I20v02 P0001 P0011 P0021 P0031 P1000 P1010 P1020 P1030 P1001 P1011 P1021 P1031 M30
M31 M32 M33 K20 I30v04 P2000 P2010 P2020 P2030 P2001 P2011 P2021 P2031 K30 K11 I21s04 I31s04 W2s K21 P3001 P3000
P3010 P3020 P3030 P3011 P3021 P3031 F001 F000 F010 F011 P0100 P1100 P0101 P2100 P1101 P0110 P2101 F021 F031 F020
K31 W3s R01v34 R01s03 T2 T3 P0111 P3100 P3101 P0131 P1111 P1131 C2s C3s W0v W1v N01 F030 F101 P0121 P2131 P1121
P3131 P2121 P2111 P3121 P1110 P3111 P2110 P0120 P0130 Q1 F131 F121 F111 W4s W5s W6s W7v T0 T1 T4 R11v04 R00s04
SN024 F100 N11 C0s C1s C4s T5 P3110 P1130 P1120 P2130 P2120 P3130 C5s W8s W9s W10s Q0 Q2 X2_1 X0_1 F110 F130
SN002 O0_1s P3120 F120 X1_1 X3_1 X4_1 W11v R10v34 R10s03 O2_1v O3_1v SN102 T6 T7 T8 T9 T11 C6s C7s N00 N10 O4_1s
C8v C9s X5_1 X0_0 X5_0 X4_0 X1_0 SO2b SO3b O0_0v O5_0v O4_0v O5_1s Q3 Q4 W12v W13v W14v SN124 X2_0 X3_0 X6_0
X6_1 C11s SO5 SO4 O1_0s O1_1s O2_0s O3_0s O6_0s O6_1s SO2a X7_0 X7_1 X8_0 W15v T10 T12 T13 T14 O7_0v O7_1s C10v
C12v C13v SO0 SO1 Q5 T15 X8_1 X9_0 X9_1 X10_0 X10_1 O8_0v O8_1s O9_0s O9_1v C14s C15s SO3a SP3 X11_0 X11_1 SO8
Q6 O10_0v O10_1s O11_0v X12_0 X12_1 X13_0 X13_1 Q7 X14_0 X14_1 X15_1 SO9 SO10 O12_0v O11_1s O12_1s O13_0v O13_1v
O15_1v X15_0 SO11 SO12 SO13 O15_0v O14_0s O14_1s SO14 SO15"""


def tile_linear_attention_state_s9_kernel(
    tc, keys, key_decay, v_words, v_scales, state, state_decay, queries, read_decay, out_0, out_1
):
    nc = tc.nc
    with ExitStack() as ctx:
        keep = ctx.enter_context(tc.tile_pool(name="keep", bufs=1))
        stage = ctx.enter_context(tc.tile_pool(name="stage", bufs=4))
        il = ctx.enter_context(tc.tile_pool(name="il", bufs=2))
        nil = ctx.enter_context(tc.tile_pool(name="nil", bufs=4))
        wpool = ctx.enter_context(tc.tile_pool(name="wpool", bufs=6))
        qpool = ctx.enter_context(tc.tile_pool(name="qpool", bufs=3))
        psum = ctx.enter_context(tc.psum_pool(name="psum", bufs=1))

        dec_rows = keep.tile([P, 512], BF16, name="dec_rows", align_bytes=64)
        dec = keep.tile([P, 10, 4], BF16, name="dec", align_bytes=64)
        kdec0 = keep.tile([P, 4], BF16, name="kdec0", align_bytes=64)
        rdec32 = keep.tile([P, 4, 4], F32, name="rdec32")
        dummy = keep.tile([P, 2], F32, name="dummy")
        vsc = keep.tile([P, TG, E], U8, name="vsc", align_bytes=64)
        ident = keep.tile([P, P], F32, name="ident", align_bytes=64)
        st = keep.tile([P, DG, 4, E], BF16, name="st", align_bytes=64)
        ns32 = keep.tile([P, DG, 4, E], F32, name="ns32", align_bytes=64)
        kd_codes = keep.tile([P, TG, D], U32, name="kd_codes", align_bytes=64)
        kd_scales = keep.tile([P, TG, D], U8, name="kd_scales", align_bytes=64)
        q_codes = keep.tile([P, LT, DG, P], U32, name="q_codes", align_bytes=64)
        q_scales = keep.tile([P, LT, DG, P], U8, name="q_scales", align_bytes=64)
        ns_codes = keep.tile([P, DG, E], U32, name="ns_codes", align_bytes=64)
        ns_scales = keep.tile([P, DG, E], U8, name="ns_scales", align_bytes=64)

        keys_v = keys.rearrange("(g p j) d -> g p j d", p=P, j=4)
        q_v = queries.rearrange("(c p r) d -> c p r d", p=P, r=4)
        st_v = state.rearrange("(b p t) e -> b p t e", p=P, t=4)
        out0_v = out_0.rearrange("(c p r) e -> c p r e", p=P, r=4)
        out1_v = out_1.rearrange("(b p t) e -> b p t e", p=P, t=4)
        kraw = []
        vw = keep.tile([P, TG, 2 * E], U8, name="vw", align_bytes=64)
        qraw = []
        for g in range(TG):
            kr = stage.tile([P, 4, D], BF16, name="raw", align_bytes=64)
            kraw.append(kr)
        for c in range(4):
            qr = keep.tile([P, 4, D], BF16, name=f"qraw{c}", align_bytes=64)
            qraw.append(qr)

        with tc.manual_schedule():
            nc.scalar.dma_start(out=kdec0[:], in_=key_decay[0:512].rearrange("(p j) -> p j", j=4))
            nc.vector.memset(dummy[:], 0.0)
            nc.vector.memset(dec_rows[:].bitcast(I32), 0)
            nc.scalar.dma_start(out=dec_rows[0:4, :], in_=key_decay.rearrange("(g n) -> g n", n=512))
            nc.scalar.dma_start(out=dec_rows[4:6, :], in_=state_decay.rearrange("(g n) -> g n", n=512))
            nc.scalar.dma_start(out=dec_rows[6:10, :], in_=read_decay.rearrange("(g n) -> g n", n=512))
            nc.vector.memset(vsc[:].rearrange("p g n -> p (g n)").bitcast(I32), 0)
            nc.scalar.activation(out=dummy[:, 1:2], in_=dummy[:, 0:1], func=COPY)
            make_identity(nc, ident[:])
            for name in LOADS.split():
                i = int(name[1:2]) if name not in ("sa", "sb", "sc") else 0
                if name in ("sa", "sb", "sc"):
                    lo, hi = {"sa": (0, 1), "sb": (1, TG), "sc": (0, TG)}[name]
                    for q in range(4):
                        nc.sync.dma_start(
                            out=vsc[32 * q : 32 * q + 4, lo:hi, :].bitcast(I32),
                            in_=v_scales[lo:hi, 4 * q : 4 * q + 4, :].rearrange("g q n -> q g n").bitcast(I32),
                        )
                elif name[0:1] in ("v", "V"):
                    end = i + 1 if name[0:1] == "v" else i + 2
                    nc.sync.dma_start(
                        out=vw[:, i:end, :].bitcast(I32), in_=v_words[i:end].rearrange("g p n -> p g n").bitcast(I32)
                    )
                elif name[0:1] == "s":
                    nc.sync.dma_start(out=st[:, i], in_=st_v[i])
                elif name[-1] in ("L", "R"):
                    cols = slice(0, 512) if name[-1] == "L" else slice(512, 1024)
                    nc.sync.dma_start(out=kraw[0][:, :, cols], in_=keys_v[0, :, :, cols])
                else:
                    tiles, view = (kraw, keys_v) if name[0:1] == "k" else (qraw, q_v)
                    rows = slice(int(name[3:4]), int(name[3:4]) + 2) if len(name) > 2 else slice(0, 4)
                    nc.sync.dma_start(out=tiles[i][:, rows, :], in_=view[i, :, rows, :])

            free_banks = list(range(8))
            bank_of = {}
            acc_of = {}
            il_of = {}
            res_of = {}

            def take(key):
                k = free_banks.pop(0)
                bank_of[key] = k
                acc = psum.tile([P, HALF], F32, name=f"bank{k}")
                acc_of[key] = acc
                return acc


            for tok in ORDER.split():
                c = tok[0:1]
                if c == "D":
                    bank = take("dec")
                    for u in range(2):
                        nc.tensor.transpose(bank[:, P * u : P * u + P], dec_rows[:].bitcast(F32)[:, u:256:2], ident[:])
                    nc.vector.tensor_copy(
                        out=dec[:].rearrange("p r j -> p (r j)").bitcast(F32).rearrange("p (r u) -> p r u", u=2),
                        in_=bank[:, 0 : 2 * P].rearrange("p (u r) -> p r u", u=2)[:, 0:10, :],
                    )
                    free_banks.append(bank_of["dec"])
                    nc.vector.tensor_copy(out=rdec32[:], in_=dec[:, 6:10, :])
                elif c == "m":
                    j, b = int(tok[1:2]), int(tok[2:3])
                    part = kraw[0][:, j, 512 * b : 512 * b + 512]
                    nc.vector.tensor_scalar(out=part, in0=part, scalar1=kdec0[:, j : j + 1], scalar2=None, op0=MULT)
                elif c == "M":
                    g, j = int(tok[1:2]), int(tok[2:3])
                    part = kraw[g][:, j, :]
                    nc.vector.tensor_scalar(out=part, in0=part, scalar1=dec[:, g, j : j + 1], scalar2=None, op0=MULT)
                elif c == "I":
                    g, b, e, lo, hi = int(tok[1:2]), int(tok[2:3]), tok[3:4], int(tok[4:5]), int(tok[5:6])
                    if (g, b) not in il_of:
                        grouped = il.tile([P, 4, P, 4], BF16, name=f"kd_il{b}", align_bytes=64)
                        il_of[(g, b)] = grouped
                    src = kraw[g][:, :, 512 * b : 512 * b + 512]
                    dst = il_of[(g, b)][:]
                    if e == "s":
                        src = src.rearrange("p j (m t) -> p m j t", t=4)[:, :, :, lo:hi]
                        dst = dst.rearrange("p t m j -> p m j t")[:, :, :, lo:hi]
                    elif hi - lo == 4:
                        src = src.rearrange("p j (m a c) -> p a m c j", a=2, c=2)
                        dst = dst.rearrange("p (a c) m j -> p a m c j", a=2)
                    else:
                        src = src.rearrange("p j (m t) -> p t m j", t=4)[:, lo:hi]
                        dst = dst[:, lo:hi]
                    if e == "s":
                        nc.scalar.copy(out=dst, in_=src)
                    else:
                        nc.vector.tensor_copy(out=dst, in_=src)
                elif c == "K":
                    g, b = int(tok[1:2]), int(tok[2:3])
                    cols = slice(512 * b, 512 * b + 512)
                    nc.vector.quantize_mx(
                        out=kd_codes[:, g, cols].bitcast(E4M3),
                        scales=kd_scales[:, g, cols],
                        in_=il_of[(g, b)][:].rearrange("p t m j -> p (t m j)"),
                    )
                elif c == "P":
                    g, b, t, h = int(tok[1:2]), int(tok[2:3]), int(tok[3:4]), int(tok[4:5])
                    key = ("a", b, t, h)
                    acc = take(key) if g == 0 else acc_of[key]
                    cols = slice(512 * b + P * t, 512 * b + P * t + P)
                    nc.tensor.matmul_mx(
                        out=acc[:],
                        lhsT=kd_codes[:, g, cols].bitcast(E4M3),
                        lhsT_scale=kd_scales[:, g, cols],
                        rhs=vw[:, g, 2 * HALF * h : 2 * HALF * (h + 1)].bitcast(E2M1),
                        rhs_scale=vsc[:, g, HALF * h : HALF * (h + 1)],
                        start=(g == 0),
                        stop=(g == TG - 1),
                    )
                elif c == "W":
                    l = int(tok[1:-1])
                    perm = wpool.tile([P, DG, 2, P], F32, name="perm", align_bytes=64)
                    il_of[("w", l)] = perm
                    src = qraw[l // 4][:, l % 4, :].bitcast(F32).rearrange("p (b r u) -> p b u r", b=DG, u=2)
                    if tok[-1] == "v":
                        nc.vector.tensor_copy(out=perm[:], in_=src)
                    else:
                        nc.scalar.copy(out=perm[:], in_=src)
                elif c == "T":
                    l = int(tok[1:])
                    words = qraw[l // 4][:, l % 4, :].bitcast(F32)
                    perm = il_of.get(("w", l))
                    bank = take(("t", l))
                    for b in range(DG):
                        for u in range(2):
                            col = P * (2 * b + u)
                            if perm is None:
                                part = words[:, 256 * b + u : 256 * (b + 1) : 2]
                            else:
                                part = perm[:, b, u, :]
                            nc.tensor.transpose(bank[:, col : col + P], part, ident[:])
                elif c == "C":
                    l, e = int(tok[1:-1]), tok[-1]
                    if ("q", l // 2) not in il_of:
                        pair = qpool.tile([P, 2, DG, P, 4], BF16, name="q_il", align_bytes=64)
                        il_of[("q", l // 2)] = pair
                    pair = il_of[("q", l // 2)]
                    dst = pair[:, l % 2].rearrange("p b r t -> p (b r t)").bitcast(F32)
                    dst = dst.rearrange("p (b r u) -> p b r u", b=DG, u=2)
                    src = acc_of[("t", l)][:].rearrange("p (b u r) -> p b r u", b=DG, u=2)
                    if e == "s":
                        nc.scalar.copy(out=dst, in_=src)
                    else:
                        nc.vector.tensor_copy(out=dst, in_=src)
                    free_banks.append(bank_of[("t", l)])
                elif c == "Q":
                    i = int(tok[1:])
                    nc.vector.quantize_mx(
                        out=q_codes[:, 2 * i : 2 * i + 2].rearrange("p l b r -> p (l b r)").bitcast(E4M3),
                        scales=q_scales[:, 2 * i : 2 * i + 2].rearrange("p l b r -> p (l b r)"),
                        in_=il_of[("q", i)][:].rearrange("p l b r t -> p (l b r t)"),
                    )
                elif c == "F":
                    b, t, h = int(tok[1:2]), int(tok[2:3]), int(tok[3:4])
                    cols = slice(HALF * h, HALF * (h + 1))
                    nc.vector.scalar_tensor_tensor(
                        out=ns32[:, b, t, cols],
                        in0=st[:, b, t, cols],
                        scalar=dec[:, 4 + b, t : t + 1],
                        in1=acc_of[("a", b, t, h)][:],
                        op0=MULT,
                        op1=ADD,
                    )
                    free_banks.append(bank_of[("a", b, t, h)])
                elif c == "R":
                    b, h, e, lo, hi = int(tok[1:2]), int(tok[2:3]), tok[3:4], int(tok[4:5]), int(tok[5:6])
                    if ("n", b, h) not in il_of:
                        grouped = nil.tile([P, HALF, 4], BF16, name="ns_il", align_bytes=64)
                        il_of[("n", b, h)] = grouped
                    dst = il_of[("n", b, h)][:, P * lo : P * hi, :]
                    src = ns32[:, b, :, HALF * h + P * lo : HALF * h + P * hi]
                    dst = dst.rearrange("p (n i) t -> p n t i", i=4)
                    src = src.rearrange("p t (n i) -> p n t i", i=4)
                    if e == "s":
                        nc.scalar.copy(out=dst, in_=src)
                    elif e == "v":
                        nc.vector.tensor_copy(out=dst, in_=src)
                    else:
                        nc.gpsimd.tensor_scalar(out=dst, in0=src, scalar1=1.0, scalar2=0.0, op0=MULT, op1=ADD)
                elif c == "N":
                    b, h = int(tok[1:2]), int(tok[2:3])
                    cols = slice(HALF * h, HALF * (h + 1))
                    nc.vector.quantize_mx(
                        out=ns_codes[:, b, cols].bitcast(E5M2),
                        scales=ns_scales[:, b, cols],
                        in_=il_of[("n", b, h)][:].rearrange("p n t -> p (n t)"),
                    )
                elif c == "X":
                    l, h = int(tok[1:].split("_")[0]), int(tok[1:].split("_")[1])
                    cols = slice(HALF * h, HALF * (h + 1))
                    acc = take(("x", l, h))
                    for b in range(DG):
                        nc.tensor.matmul_mx(
                            out=acc[:],
                            lhsT=q_codes[:, l, b, :].bitcast(E4M3),
                            lhsT_scale=q_scales[:, l, b, :],
                            rhs=ns_codes[:, b, cols].bitcast(E5M2),
                            rhs_scale=ns_scales[:, b, cols],
                            start=(b == 0),
                            stop=(b == DG - 1),
                        )
                elif c == "O":
                    l, h, e = int(tok[1:].split("_")[0]), int(tok[-2:-1]), tok[-1]
                    cols = slice(HALF * h, HALF * (h + 1))
                    if l // 2 not in res_of:
                        res = stage.tile([P, 2, E], F32, name="raw", align_bytes=64)
                        res_of[l // 2] = res
                    factor = rdec32[:, l // 4, l % 4 : l % 4 + 1]
                    if e == "s":
                        nc.scalar.activation(out=res_of[l // 2][:, l % 2, cols], in_=acc_of[("x", l, h)][:], func=COPY, scale=factor)
                    else:
                        nc.vector.tensor_scalar(
                            out=res_of[l // 2][:, l % 2, cols], in0=acc_of[("x", l, h)][:], scalar1=factor, scalar2=None, op0=MULT
                        )
                    free_banks.append(bank_of[("x", l, h)])
                elif tok[0:2] == "SP":
                    i = int(tok[2:])
                    nc.sync.dma_start(out=out0_v[i // 2, :, 2 * (i % 2) : 2 * (i % 2) + 2, :], in_=res_of[i][:])
                elif tok[0:2] == "SH":
                    b, h = int(tok[2:3]), int(tok[3:4])
                    cols = slice(HALF * h, HALF * (h + 1))
                    nc.sync.dma_start(out=out1_v[b, :, :, cols], in_=ns32[:, b, :, cols])
                elif tok[0:2] == "SO":
                    l = int(tok[2:].replace("a", "").replace("b", ""))
                    cols = slice(0, E)
                    if tok[-1] in ("a", "b"):
                        cols = slice(0, HALF) if tok[-1] == "a" else slice(HALF, E)
                    nc.sync.dma_start(out=out0_v[l // 4, :, l % 4, cols], in_=res_of[l // 2][:, l % 2, cols])
                else:
                    b, lo, hi = int(tok[2:3]), int(tok[3:4]), int(tok[4:5])
                    nc.sync.dma_start(out=out1_v[b, :, lo:hi, :], in_=ns32[:, b, lo:hi, :])
